import numpy as np
import ml_dtypes


def mxq(x, axis, fmt="e4m3"):
    dtype, down = {"e4m3": (ml_dtypes.float8_e4m3fn, 7), "e5m2": (ml_dtypes.float8_e5m2, 14)}[fmt]
    v = np.moveaxis(np.asarray(x, np.float32).astype(ml_dtypes.bfloat16).astype(np.float64), axis, -1)
    blocks = v.reshape(v.shape[:-1] + (-1, 32))
    amax = np.abs(blocks).max(-1, keepdims=True)
    byte = np.maximum(np.where(amax > 0, np.frexp(amax)[1] - 1 + 127, 0) - down, 1)
    scale = np.exp2(byte - 127.0)
    codes = (blocks / scale).astype(np.float32).astype(dtype).astype(np.float64)
    return np.moveaxis((codes * scale).reshape(v.shape), -1, axis)


WIDE = False


def mx_kscale(k):
    if not WIDE:
        return np.ones(k)
    levels = np.array([10, -10, 5, -5, 0])
    if k % 512:
        return np.exp2(np.random.permutation(np.resize(levels, k // 32))).repeat(32)
    a = np.empty((k // 512, 16))
    for p in range(k // 512):
        a[p, :8] = np.random.permutation(np.resize(levels, 8))
        for g in range(8):
            far = levels[np.abs(levels - a[p, g]) >= 10]
            a[p, g + 8] = far[np.random.randint(len(far))]
    return np.exp2(a.ravel()).repeat(32)


def f64(x):
    return np.asarray(x).astype(np.float64)


def striped(idx):
    return np.tile(idx.reshape(-1, 16).T, (8, 1)).astype(np.uint16)


def unstriped(offs):
    return offs[:16].T.reshape(-1).astype(np.int64)


def striped8(idx):
    return np.concatenate([x.reshape(-1, 16).T for x in idx]).astype(np.uint16)


def runs(offs, k):
    lists = np.stack([offs[16 * r : 16 * r + 16].T.reshape(-1) for r in range(8)]).astype(np.int64)
    return lists[np.arange(k) % 512 // 64]


def pack_weight(w):
    k, n = w.shape
    w = f64(np.asarray(w, np.float32).astype(ml_dtypes.bfloat16)).reshape(k // 32, 32, n)
    amax = np.abs(w).max(1)
    byte = np.clip(np.where(amax > 0, np.frexp(amax)[1] - 1 + 127 - 7, 1), 1, 254)
    scaled = (w * np.exp2(127.0 - byte)[:, None, :]).reshape(k, n).astype(np.float32)
    words = np.ascontiguousarray(scaled.reshape(k // 512, 128, 4, n).transpose(0, 1, 3, 2)).astype(ml_dtypes.float8_e4m3fn).view(np.uint8)
    return words, np.ascontiguousarray(byte.astype(np.uint8).reshape(k // 512, 16, n))


def unpack_weight(words, scales):
    g, p, n, _ = words.shape
    vals = np.ascontiguousarray(words).view(ml_dtypes.float8_e4m3fn).astype(np.float64) * np.repeat(np.exp2(scales.astype(np.float64) - 127.0), 8, axis=1)[..., None]
    return vals.transpose(0, 1, 3, 2).reshape(g * 512, n)


K, T, S, N, H, W = 512, 2048, 256, 512, 512, 1024


def setup_inputs():
    n = np.random.standard_normal
    s = mx_kscale(K)[:, None]
    u = mx_kscale(H)
    packed_xT = pack_weight(n((K, T)) * s)
    return {
        "x_words": packed_xT[0],
        "x_scales": packed_xT[1],
        "w1": (n((K, H)) / np.sqrt(K) / s).astype(np.float32),
        "gn": (np.random.uniform(0.5, 1.5, (H, 1)) * u[:, None]).astype(np.float32),
        "w2": (n((H, N)) / np.sqrt(2 * H) / u[:, None]).astype(np.float32),
        "w3": (n((K, N)) / np.sqrt(2 * K) / s).astype(np.float32),
        "offs": striped(np.random.permutation(T)[:S]),
        "n1": striped(np.random.randint(0, S, W)),
        "two": striped(np.random.permutation(T)[:S]),
        "n2": striped8(np.stack([np.random.permutation(S) for _ in range(8)])),
        "n3": striped8(np.stack([np.random.permutation(S) for _ in range(8)])),
    }


def reference(x_words, x_scales, w1, gn, w2, w3, offs, n1, two, n2, n3):
    xq = unpack_weight(x_words, x_scales)[:, unstriped(offs)]
    y = mxq(f64(w1), 0, "e4m3").T @ xq
    mb = y[:, unstriped(n1)]
    mn = mb.reshape(H, S, 4).min(axis=2)
    mx = mb.reshape(H, S, 4).max(axis=2)
    z = f64(gn) * (np.maximum(y, mn) - (0.5 * mx))
    x_two = unpack_weight(x_words, x_scales)[:, unstriped(two)]
    h = mxq(f64(w2), 0, "e4m3").T @ mxq(z, 0, "e4m3") + mxq(f64(w3), 0, "e4m3").T @ x_two
    st = np.maximum(h, h[np.arange(N)[:, None], runs(n2, N)])
    return np.minimum(st, st[np.arange(N)[:, None], runs(n3, N)])

@@ -1,0 +1,209 @@
+from contextlib import ExitStack
+
+import concourse.mybir as mybir
+
+K, T, S, N, H, W = 512, 2048, 256, 512, 512, 1024
+FLOPS = 3 * 2 * 512 * 512 * 256
+
+F32 = mybir.dt.float32
+BF16 = mybir.dt.bfloat16
+I32 = mybir.dt.int32
+U32 = mybir.dt.uint32
+U16 = mybir.dt.uint16
+U8 = mybir.dt.uint8
+FP8X4 = mybir.dt.float8_e4m3fn_x4
+ALU = mybir.AluOpType
+COPY = mybir.ActivationFunctionType.Copy
+
+P = 128
+PACK = 4
+MEMBERS = 4
+Y_WINDOW = 528
+H_WINDOW = 512
+W1_ON_SCALAR = 48
+
+
+def deal(engine_copy, dealt, raw, ms, ts):
+    engine_copy(
+        dealt[:, :, ms, :].rearrange("p t m j -> p m j t"),
+        raw[:].rearrange("p j (m t) -> p m j t", t=PACK)[:, ms, :, ts],
+    )
+
+
+def tile_picked_mixingmidhopmn_none_p_kernel(
+    tc, x_words, x_scales, w1, gn, w2, w3, offs, n1, two, n2, n3, out
+):
+    nc = tc.nc
+
+    def scalar_copy(dst, src):
+        nc.scalar.activation(dst, src, COPY)
+
+    with ExitStack() as ctx:
+        keep = ctx.enter_context(tc.tile_pool(name="keep", bufs=1))
+        psum = ctx.enter_context(tc.psum_pool(name="psum", bufs=1))
+
+        offs_t = keep.tile([P, S // 16], U16, name="offs_t")
+        two_t = keep.tile([P, S // 16], U16, name="two_t")
+        n1_t = keep.tile([P, W // 16], U16, name="n1_t")
+        n2_t = keep.tile([P, S // 16], U16, name="n2_t")
+        n3_t = keep.tile([P, S // 16], U16, name="n3_t")
+        words = keep.tile([P, T], U32, name="words", align_bytes=64)
+        scales = keep.tile([P, T], U8, name="scales", align_bytes=64)
+        gain = keep.tile([P, PACK], F32, name="gain")
+        w1_raw = keep.tile([P, PACK, H], F32, name="w1_raw", align_bytes=64)
+        w2_raw = keep.tile([P, PACK, N], F32, name="w2_raw", align_bytes=64)
+        w3_raw = keep.tile([P, PACK, N], F32, name="w3_raw", align_bytes=64)
+
+        y_win = [keep.tile([P, Y_WINDOW], F32, name=f"y_win{t}", align_bytes=64) for t in range(PACK)]
+        h_win = [keep.tile([P, H_WINDOW], F32, name=f"h_win{t}", align_bytes=64) for t in range(PACK)]
+        st_win = [keep.tile([P, H_WINDOW], F32, name=f"st_win{t}", align_bytes=64) for t in range(PACK)]
+
+        nc.vector.memset(scales[:].bitcast(I32), 0)
+        nc.sync.dma_start(w1_raw[:], w1.rearrange("(p j) c -> p j c", j=PACK))
+        for q in range(4):
+            nc.scalar.dma_start(
+                scales[32 * q : 32 * q + 4, :].bitcast(I32), x_scales[0, 4 * q : 4 * q + 4, :].bitcast(I32)
+            )
+        nc.sync.dma_start(offs_t[:], offs)
+        nc.sync.dma_start(words[:].bitcast(I32), x_words[0].rearrange("p n t -> p (n t)").bitcast(I32))
+        nc.sync.dma_start(two_t[:], two)
+        nc.sync.dma_start(n1_t[:], n1)
+        nc.sync.dma_start(w3_raw[:], w3.rearrange("(p j) c -> p j c", j=PACK))
+        nc.sync.dma_start(w2_raw[:], w2.rearrange("(p j) c -> p j c", j=PACK))
+        nc.sync.dma_start(gain[:], gn.rearrange("(p t) o -> p (t o)", t=PACK))
+        nc.sync.dma_start(n2_t[:], n2)
+        nc.sync.dma_start(n3_t[:], n3)
+
+        for t in range(PACK):
+            nc.vector.memset(y_win[t][:, S:], 0.0)
+        for t in range(PACK):
+            nc.gpsimd.memset(h_win[t][:, S:], 0.0)
+            nc.gpsimd.memset(st_win[t][:, S:], 0.0)
+
+        w1_bf = keep.tile([P, PACK, P, PACK], BF16, name="w1_bf", align_bytes=64)
+        deal(scalar_copy, w1_bf, w1_raw, slice(0, W1_ON_SCALAR), slice(0, PACK))
+        deal(nc.vector.tensor_copy, w1_bf, w1_raw, slice(W1_ON_SCALAR, P), slice(0, PACK))
+        w1_c = keep.tile([P, H], U32, name="w1_c", align_bytes=64)
+        w1_s = keep.tile([P, H], U8, name="w1_s", align_bytes=64)
+
+        pw = [keep.tile([P, S], U32, name=f"pw{i}", align_bytes=64) for i in range(2)]
+        ps = [keep.tile([P, S], U8, name=f"ps{i}", align_bytes=64) for i in range(2)]
+        nc.vector.tensor_copy(ps[0][:], scales[:].indirect(offs_t[:]))
+        nc.vector.quantize_mx(w1_c[:].bitcast(FP8X4), w1_s[:], w1_bf[:].rearrange("p t m j -> p (t m j)"))
+        nc.vector.tensor_copy(ps[1][:], scales[:].indirect(two_t[:]))
+        nc.vector.tensor_copy(pw[0][:], words[:].indirect(offs_t[:]))
+        nc.vector.tensor_copy(pw[1][:], words[:].indirect(two_t[:]))
+
+        y_ps = [psum.tile([P, S], F32, name=f"y_ps{t}") for t in range(PACK)]
+        for t in range(PACK):
+            cols = slice(t * P, (t + 1) * P)
+            nc.tensor.matmul_mx(
+                y_ps[t][:], w1_c[:, cols].bitcast(FP8X4), w1_s[:, cols],
+                pw[0][:].bitcast(FP8X4), ps[0][:], start=True, stop=True,
+            )
+        scalar_copy(y_win[0][:, :S], y_ps[0][:])
+        for t in range(1, PACK):
+            nc.vector.tensor_copy(y_win[t][:, :S], y_ps[t][:])
+
+        members = [keep.tile([P, S, MEMBERS], F32, name=f"members{t}", align_bytes=64) for t in range(PACK)]
+        for t in range(PACK):
+            for i in range(2):
+                nc.scalar.activation(
+                    members[t][:, i * (S // 2) : (i + 1) * (S // 2), :].rearrange("p j a -> p (j a)"),
+                    y_win[t][:].indirect(n1_t[:, i * 32 : (i + 1) * 32]),
+                    COPY,
+                )
+
+        u = keep.tile([P, PACK, S], F32, name="u", align_bytes=64)
+        lo = [keep.tile([P, S, 2], F32, name=f"lo{t}", align_bytes=64) for t in range(PACK)]
+        hi = [keep.tile([P, S, 2], F32, name=f"hi{t}", align_bytes=64) for t in range(PACK)]
+        mn = [keep.tile([P, S], F32, name=f"mn{t}", align_bytes=64) for t in range(PACK)]
+        mx = [keep.tile([P, S], F32, name=f"mx{t}", align_bytes=64) for t in range(PACK)]
+        top = [keep.tile([P, S], F32, name=f"top{t}", align_bytes=64) for t in range(PACK)]
+
+        def combine(t):
+            nc.vector.scalar_tensor_tensor(u[:, t, :], mx[t][:], -0.5, top[t][:], ALU.mult, ALU.add)
+
+        for t in range(PACK):
+            m = members[t]
+            pieces = [slice(0, S // 2), slice(S // 2, S)] if t == 0 else [slice(0, S)]
+            for js in pieces:
+                nc.vector.tensor_tensor(lo[t][:, js, :], m[:, js, 0:2], m[:, js, 2:4], ALU.min)
+                if t > 0:
+                    combine(t - 1)
+                nc.vector.tensor_tensor(hi[t][:, js, :], m[:, js, 0:2], m[:, js, 2:4], ALU.max)
+            nc.vector.tensor_tensor(mn[t][:], lo[t][:, :, 0], lo[t][:, :, 1], ALU.min)
+            nc.vector.tensor_tensor(mx[t][:], hi[t][:, :, 0], hi[t][:, :, 1], ALU.max)
+            nc.vector.tensor_tensor(top[t][:], mn[t][:], y_win[t][:, :S], ALU.max)
+
+        w_bf, w_c, w_s = {}, {}, {}
+        for half in range(2):
+            for nm, raw in (("w3", w3_raw), ("w2", w2_raw)):
+                w_bf[nm, half] = keep.tile([P, 2, P, PACK], BF16, name=f"{nm}_bf{half}", align_bytes=64)
+                w_c[nm, half] = keep.tile([P, 2 * P], U32, name=f"{nm}_c{half}", align_bytes=64)
+                w_s[nm, half] = keep.tile([P, 2 * P], U8, name=f"{nm}_s{half}", align_bytes=64)
+                deal(scalar_copy, w_bf[nm, half], raw, slice(0, P), slice(2 * half, 2 * half + 2))
+
+        def quantize_weight(nm, half):
+            nc.vector.quantize_mx(
+                w_c[nm, half][:].bitcast(FP8X4), w_s[nm, half][:], w_bf[nm, half][:].rearrange("p t m j -> p (t m j)")
+            )
+
+        quantize_weight("w3", 0)
+        combine(PACK - 1)
+        quantize_weight("w2", 0)
+
+        z_bf = keep.tile([P, S, PACK], BF16, name="z_bf", align_bytes=64)
+        nc.vector.tensor_tensor(
+            z_bf[:].rearrange("p (c i) t -> p c t i", i=4),
+            u[:].rearrange("p t (c i) -> p c t i", i=4),
+            gain[:].unsqueeze(1).unsqueeze(3).to_broadcast([P, S // 4, PACK, 4]),
+            ALU.mult,
+        )
+        z_c = keep.tile([P, S], U32, name="z_c", align_bytes=64)
+        z_s = keep.tile([P, S], U8, name="z_s", align_bytes=64)
+        nc.vector.quantize_mx(z_c[:].bitcast(FP8X4), z_s[:], z_bf[:].rearrange("p j t -> p (j t)"))
+
+        out_rows = out.rearrange("(p t) j -> p t j", t=PACK)
+        h_ps = [psum.tile([P, S], F32, name=f"h_ps{t}") for t in range(PACK)]
+
+        def product(t):
+            half = t // 2
+            cols = slice((t % 2) * P, (t % 2 + 1) * P)
+            nc.tensor.matmul_mx(
+                h_ps[t][:], w_c["w3", half][:, cols].bitcast(FP8X4), w_s["w3", half][:, cols],
+                pw[1][:].bitcast(FP8X4), ps[1][:], start=True, stop=False,
+            )
+            nc.tensor.matmul_mx(
+                h_ps[t][:], w_c["w2", half][:, cols].bitcast(FP8X4), w_s["w2", half][:, cols],
+                z_c[:].bitcast(FP8X4), z_s[:], start=False, stop=True,
+            )
+            nc.vector.tensor_copy(h_win[t][:, :S], h_ps[t][:])
+
+        h_at = [keep.tile([P, S], F32, name=f"h_at{t}", align_bytes=64) for t in range(PACK)]
+        st_at = [keep.tile([P, S], F32, name=f"st_at{t}", align_bytes=64) for t in range(PACK)]
+        res = [keep.tile([P, S], F32, name=f"res{t}", align_bytes=64) for t in range(PACK)]
+
+        def first_hop(t):
+            nc.scalar.activation(h_at[t][:], h_win[t][:].indirect(n2_t[:]), COPY)
+            nc.vector.tensor_tensor(st_win[t][:, :S], h_win[t][:, :S], h_at[t][:], ALU.max)
+
+        def second_hop(t):
+            nc.scalar.activation(st_at[t][:], st_win[t][:].indirect(n3_t[:]), COPY)
+            nc.vector.tensor_tensor(res[t][:], st_win[t][:, :S], st_at[t][:], ALU.min)
+            nc.sync.dma_start(out_rows[:, t, :], res[t][:])
+
+        quantize_weight("w3", 1)
+        product(0)
+        product(1)
+        quantize_weight("w2", 1)
+        first_hop(0)
+        product(2)
+        first_hop(1)
+        product(3)
+        second_hop(0)
+        first_hop(2)
+        second_hop(1)
+        first_hop(3)
+        second_hop(2)
+        second_hop(3)

@@ -49,50 +49,49 @@ def tile_picked_mixingmidhopmn_none_p_kernel(
         n3_t = keep.tile([P, S // 16], U16, name="n3_t")
         words = keep.tile([P, T], U32, name="words", align_bytes=64)
         scales = keep.tile([P, T], U8, name="scales", align_bytes=64)
-        gain = keep.tile([P, PACK], F32, name="gain")
-        w1_raw = keep.tile([P, PACK, H], F32, name="w1_raw", align_bytes=64)
-        w2_raw = keep.tile([P, PACK, N], F32, name="w2_raw", align_bytes=64)
-        w3_raw = keep.tile([P, PACK, N], F32, name="w3_raw", align_bytes=64)
+        w1_raw = keep.tile([P, PACK, H], F32, name="w1_raw", tag="first", align_bytes=64)
 
         y_win = [keep.tile([P, Y_WINDOW], F32, name=f"y_win{t}", align_bytes=64) for t in range(PACK)]
         h_win = [keep.tile([P, H_WINDOW], F32, name=f"h_win{t}", align_bytes=64) for t in range(PACK)]
         st_win = [keep.tile([P, H_WINDOW], F32, name=f"st_win{t}", align_bytes=64) for t in range(PACK)]
 
-        nc.vector.memset(scales[:].bitcast(I32), 0)
-        nc.sync.dma_start(w1_raw[:], w1.rearrange("(p j) c -> p j c", j=PACK))
-        for q in range(4):
-            nc.scalar.dma_start(
-                scales[32 * q : 32 * q + 4, :].bitcast(I32), x_scales[0, 4 * q : 4 * q + 4, :].bitcast(I32)
-            )
+        scale_rows = keep.tile([P, T], U8, name="scale_rows", tag="small", align_bytes=64)
+        for r in range(4):
+            nc.sync.dma_start(scale_rows[r:P:32, :].bitcast(I32), x_scales[0, r:16:4, :].bitcast(I32))
         nc.sync.dma_start(offs_t[:], offs)
-        nc.sync.dma_start(words[:].bitcast(I32), x_words[0].rearrange("p n t -> p (n t)").bitcast(I32))
+        nc.sync.dma_start(w1_raw[:], w1.rearrange("(p j) c -> p j c", j=PACK))
         nc.sync.dma_start(two_t[:], two)
+        nc.sync.dma_start(words[:].bitcast(I32), x_words[0].rearrange("p n t -> p (n t)").bitcast(I32))
         nc.sync.dma_start(n1_t[:], n1)
-        nc.sync.dma_start(w3_raw[:], w3.rearrange("(p j) c -> p j c", j=PACK))
-        nc.sync.dma_start(w2_raw[:], w2.rearrange("(p j) c -> p j c", j=PACK))
-        nc.sync.dma_start(gain[:], gn.rearrange("(p t) o -> p (t o)", t=PACK))
         nc.sync.dma_start(n2_t[:], n2)
         nc.sync.dma_start(n3_t[:], n3)
 
+        nc.vector.memset(scales[:].bitcast(I32), 0)
+        for q in range(4):
+            rows = slice(32 * q, 32 * q + 4)
+            nc.vector.tensor_copy(scales[rows, :].bitcast(I32), scale_rows[rows, :].bitcast(I32))
+        ps = [keep.tile([P, S], U8, name=f"ps{i}", align_bytes=64) for i in range(2)]
+        nc.vector.tensor_copy(ps[0][:], scales[:].indirect(offs_t[:]))
+        nc.vector.tensor_copy(ps[1][:], scales[:].indirect(two_t[:]))
+
         for t in range(PACK):
             nc.vector.memset(y_win[t][:, S:], 0.0)
-        for t in range(PACK):
-            nc.gpsimd.memset(h_win[t][:, S:], 0.0)
-            nc.gpsimd.memset(st_win[t][:, S:], 0.0)
 
-        w1_bf = keep.tile([P, PACK, P, PACK], BF16, name="w1_bf", align_bytes=64)
+        w1_bf = keep.tile([P, PACK, P, PACK], BF16, name="w1_bf", tag="second", align_bytes=64)
         deal(scalar_copy, w1_bf, w1_raw, slice(0, W1_ON_SCALAR), slice(0, PACK))
         deal(nc.vector.tensor_copy, w1_bf, w1_raw, slice(W1_ON_SCALAR, P), slice(0, PACK))
         w1_c = keep.tile([P, H], U32, name="w1_c", align_bytes=64)
         w1_s = keep.tile([P, H], U8, name="w1_s", align_bytes=64)
+        nc.vector.quantize_mx(w1_c[:].bitcast(FP8X4), w1_s[:], w1_bf[:].rearrange("p t m j -> p (t m j)"))
 
         pw = [keep.tile([P, S], U32, name=f"pw{i}", align_bytes=64) for i in range(2)]
-        ps = [keep.tile([P, S], U8, name=f"ps{i}", align_bytes=64) for i in range(2)]
-        nc.vector.tensor_copy(ps[0][:], scales[:].indirect(offs_t[:]))
-        nc.vector.quantize_mx(w1_c[:].bitcast(FP8X4), w1_s[:], w1_bf[:].rearrange("p t m j -> p (t m j)"))
-        nc.vector.tensor_copy(ps[1][:], scales[:].indirect(two_t[:]))
         nc.vector.tensor_copy(pw[0][:], words[:].indirect(offs_t[:]))
         nc.vector.tensor_copy(pw[1][:], words[:].indirect(two_t[:]))
+
+        w3_raw = keep.tile([P, PACK, N], F32, name="w3_raw", tag="first", align_bytes=64)
+        w2_raw = keep.tile([P, PACK, N], F32, name="w2_raw", tag="second", align_bytes=64)
+        nc.sync.dma_start(w3_raw[:], w3.rearrange("(p j) c -> p j c", j=PACK))
+        nc.sync.dma_start(w2_raw[:], w2.rearrange("(p j) c -> p j c", j=PACK))
 
         y_ps = [psum.tile([P, S], F32, name=f"y_ps{t}") for t in range(PACK)]
         for t in range(PACK):
@@ -105,6 +104,9 @@ def tile_picked_mixingmidhopmn_none_p_kernel(
         for t in range(1, PACK):
             nc.vector.tensor_copy(y_win[t][:, :S], y_ps[t][:])
 
+        gain = keep.tile([P, PACK], F32, name="gain", tag="small", align_bytes=64)
+        nc.sync.dma_start(gain[:], gn.rearrange("(p t) o -> p (t o)", t=PACK))
+
         members = [keep.tile([P, S, MEMBERS], F32, name=f"members{t}", align_bytes=64) for t in range(PACK)]
         for t in range(PACK):
             for i in range(2):
@@ -114,55 +116,93 @@ def tile_picked_mixingmidhopmn_none_p_kernel(
                     COPY,
                 )
 
-        u = keep.tile([P, PACK, S], F32, name="u", align_bytes=64)
+        halves = (slice(0, S // 2), slice(S // 2, S))
         lo = [keep.tile([P, S, 2], F32, name=f"lo{t}", align_bytes=64) for t in range(PACK)]
         hi = [keep.tile([P, S, 2], F32, name=f"hi{t}", align_bytes=64) for t in range(PACK)]
         mn = [keep.tile([P, S], F32, name=f"mn{t}", align_bytes=64) for t in range(PACK)]
-        mx = [keep.tile([P, S], F32, name=f"mx{t}", align_bytes=64) for t in range(PACK)]
+        mx = [h_win[t][:, S:] for t in range(PACK)]
         top = [keep.tile([P, S], F32, name=f"top{t}", align_bytes=64) for t in range(PACK)]
-
-        def combine(t):
-            nc.vector.scalar_tensor_tensor(u[:, t, :], mx[t][:], -0.5, top[t][:], ALU.mult, ALU.add)
-
-        for t in range(PACK):
-            m = members[t]
-            pieces = [slice(0, S // 2), slice(S // 2, S)] if t == 0 else [slice(0, S)]
-            for js in pieces:
-                nc.vector.tensor_tensor(lo[t][:, js, :], m[:, js, 0:2], m[:, js, 2:4], ALU.min)
-                if t > 0:
-                    combine(t - 1)
-                nc.vector.tensor_tensor(hi[t][:, js, :], m[:, js, 0:2], m[:, js, 2:4], ALU.max)
-            nc.vector.tensor_tensor(mn[t][:], lo[t][:, :, 0], lo[t][:, :, 1], ALU.min)
-            nc.vector.tensor_tensor(mx[t][:], hi[t][:, :, 0], hi[t][:, :, 1], ALU.max)
-            nc.vector.tensor_tensor(top[t][:], mn[t][:], y_win[t][:, :S], ALU.max)
+        u = keep.tile([P, PACK, S], F32, name="u", align_bytes=64)
 
         w_bf, w_c, w_s = {}, {}, {}
-        for half in range(2):
-            for nm, raw in (("w3", w3_raw), ("w2", w2_raw)):
-                w_bf[nm, half] = keep.tile([P, 2, P, PACK], BF16, name=f"{nm}_bf{half}", align_bytes=64)
-                w_c[nm, half] = keep.tile([P, 2 * P], U32, name=f"{nm}_c{half}", align_bytes=64)
-                w_s[nm, half] = keep.tile([P, 2 * P], U8, name=f"{nm}_s{half}", align_bytes=64)
-                deal(scalar_copy, w_bf[nm, half], raw, slice(0, P), slice(2 * half, 2 * half + 2))
 
-        def quantize_weight(nm, half):
+        def round_weight(engine_copy, nm, raw, half):
+            w_bf[nm, half] = keep.tile([P, 2, P, PACK], BF16, name=f"{nm}_bf{half}", align_bytes=64)
+            deal(engine_copy, w_bf[nm, half], raw, slice(0, P), slice(2 * half, 2 * half + 2))
+
+        def quantize_weight(nm, half, tag):
+            w_c[nm, half] = keep.tile([P, 2 * P], U32, name=f"{nm}_c{half}", tag=tag, align_bytes=64)
+            w_s[nm, half] = keep.tile([P, 2 * P], U8, name=f"{nm}_s{half}", align_bytes=64)
             nc.vector.quantize_mx(
                 w_c[nm, half][:].bitcast(FP8X4), w_s[nm, half][:], w_bf[nm, half][:].rearrange("p t m j -> p (t m j)")
             )
 
-        quantize_weight("w3", 0)
-        combine(PACK - 1)
-        quantize_weight("w2", 0)
+        def pair_min(t, js):
+            nc.vector.tensor_tensor(lo[t][:, js, :], members[t][:, js, 0:2], members[t][:, js, 2:4], ALU.min)
 
-        z_bf = keep.tile([P, S, PACK], BF16, name="z_bf", align_bytes=64)
-        nc.vector.tensor_tensor(
-            z_bf[:].rearrange("p (c i) t -> p c t i", i=4),
-            u[:].rearrange("p t (c i) -> p c t i", i=4),
-            gain[:].unsqueeze(1).unsqueeze(3).to_broadcast([P, S // 4, PACK, 4]),
-            ALU.mult,
-        )
-        z_c = keep.tile([P, S], U32, name="z_c", align_bytes=64)
-        z_s = keep.tile([P, S], U8, name="z_s", align_bytes=64)
-        nc.vector.quantize_mx(z_c[:].bitcast(FP8X4), z_s[:], z_bf[:].rearrange("p j t -> p (j t)"))
+        def pair_max(t, js):
+            nc.vector.tensor_tensor(hi[t][:, js, :], members[t][:, js, 0:2], members[t][:, js, 2:4], ALU.max)
+
+        def extremes(t, js):
+            nc.vector.tensor_tensor(mn[t][:, js], lo[t][:, js, 0], lo[t][:, js, 1], ALU.min)
+            nc.vector.tensor_tensor(mx[t][:, js], hi[t][:, js, 0], hi[t][:, js, 1], ALU.max)
+
+        def larger(t, js):
+            nc.vector.tensor_tensor(top[t][:, js], mn[t][:, js], y_win[t][:, js], ALU.max)
+
+        def combine(t, js):
+            nc.vector.scalar_tensor_tensor(u[:, t, js], mx[t][:, js], -0.5, top[t][:, js], ALU.mult, ALU.add)
+
+        z_bf = [keep.tile([P, S // 2, PACK], BF16, name=f"z_bf{i}", tag=f"z_bf{i}", align_bytes=64) for i in range(2)]
+        z_c = [keep.tile([P, S // 2], U32, name=f"z_c{i}", align_bytes=64) for i in range(2)]
+        z_s = [keep.tile([P, S // 2], U8, name=f"z_s{i}", align_bytes=64) for i in range(2)]
+
+        def round_z(i):
+            nc.vector.tensor_tensor(
+                z_bf[i][:].rearrange("p (c i) t -> p c t i", i=4),
+                u[:, :, halves[i]].rearrange("p t (c i) -> p c t i", i=4),
+                gain[:].unsqueeze(1).unsqueeze(3).to_broadcast([P, S // 8, PACK, 4]),
+                ALU.mult,
+            )
+
+        def quantize_z(i):
+            nc.vector.quantize_mx(z_c[i][:].bitcast(FP8X4), z_s[i][:], z_bf[i][:].rearrange("p j t -> p (j t)"))
+
+        whole = slice(0, S)
+        last = PACK - 1
+        for t in range(last):
+            pair_min(t, halves[0])
+            pair_max(t, halves[0])
+            if t == 0:
+                round_weight(nc.vector.tensor_copy, "w3", w3_raw, 0)
+            else:
+                combine(t - 1, whole)
+            pair_min(t, halves[1])
+            pair_max(t, halves[1])
+            if t == 0:
+                quantize_weight("w3", 0, "w3_c0")
+            extremes(t, whole)
+            larger(t, whole)
+        round_weight(scalar_copy, "w2", w2_raw, 0)
+        round_weight(scalar_copy, "w3", w3_raw, 1)
+        round_weight(scalar_copy, "w2", w2_raw, 1)
+        first, second = halves
+        pair_min(last, first)
+        pair_max(last, first)
+        combine(last - 1, whole)
+        extremes(last, first)
+        pair_min(last, second)
+        larger(last, first)
+        pair_max(last, second)
+        combine(last, first)
+        extremes(last, second)
+        round_z(0)
+        larger(last, second)
+        quantize_z(0)
+        combine(last, second)
+        quantize_weight("w2", 0, "w2_c")
+        round_z(1)
+        quantize_z(1)
 
         out_rows = out.rearrange("(p t) j -> p t j", t=PACK)
         h_ps = [psum.tile([P, S], F32, name=f"h_ps{t}") for t in range(PACK)]
@@ -174,36 +214,39 @@ def tile_picked_mixingmidhopmn_none_p_kernel(
                 h_ps[t][:], w_c["w3", half][:, cols].bitcast(FP8X4), w_s["w3", half][:, cols],
                 pw[1][:].bitcast(FP8X4), ps[1][:], start=True, stop=False,
             )
-            nc.tensor.matmul_mx(
-                h_ps[t][:], w_c["w2", half][:, cols].bitcast(FP8X4), w_s["w2", half][:, cols],
-                z_c[:].bitcast(FP8X4), z_s[:], start=False, stop=True,
-            )
+            for i in range(2):
+                nc.tensor.matmul_mx(
+                    h_ps[t][:, halves[i]], w_c["w2", half][:, cols].bitcast(FP8X4), w_s["w2", half][:, cols],
+                    z_c[i][:].bitcast(FP8X4), z_s[i][:], start=False, stop=(i == 1),
+                )
             nc.vector.tensor_copy(h_win[t][:, :S], h_ps[t][:])
 
-        h_at = [keep.tile([P, S], F32, name=f"h_at{t}", align_bytes=64) for t in range(PACK)]
+        h_at = [st_win[t][:, S:] for t in range(PACK)]
         st_at = [keep.tile([P, S], F32, name=f"st_at{t}", align_bytes=64) for t in range(PACK)]
         res = [keep.tile([P, S], F32, name=f"res{t}", align_bytes=64) for t in range(PACK)]
 
         def first_hop(t):
-            nc.scalar.activation(h_at[t][:], h_win[t][:].indirect(n2_t[:]), COPY)
-            nc.vector.tensor_tensor(st_win[t][:, :S], h_win[t][:, :S], h_at[t][:], ALU.max)
+            nc.scalar.activation(h_at[t], h_win[t][:].indirect(n2_t[:]), COPY)
+            nc.vector.tensor_tensor(st_win[t][:, :S], h_win[t][:, :S], h_at[t], ALU.max)
 
-        def second_hop(t):
-            nc.scalar.activation(st_at[t][:], st_win[t][:].indirect(n3_t[:]), COPY)
-            nc.vector.tensor_tensor(res[t][:], st_win[t][:, :S], st_at[t][:], ALU.min)
-            nc.sync.dma_start(out_rows[:, t, :], res[t][:])
+        def second_hop(t, js):
+            offsets = n3_t[:, js.start // 16 : js.stop // 16]
+            nc.scalar.activation(st_at[t][:, js], st_win[t][:].indirect(offsets), COPY)
+            nc.vector.tensor_tensor(res[t][:, js], st_win[t][:, js], st_at[t][:, js], ALU.min)
+            nc.sync.dma_start(out_rows[:, t, js], res[t][:, js])
 
-        quantize_weight("w3", 1)
+        quantize_weight("w3", 1, "z_bf1")
         product(0)
         product(1)
-        quantize_weight("w2", 1)
+        quantize_weight("w2", 1, "w2_c")
         first_hop(0)
         product(2)
         first_hop(1)
         product(3)
-        second_hop(0)
+        second_hop(0, whole)
         first_hop(2)
-        second_hop(1)
+        second_hop(1, whole)
         first_hop(3)
-        second_hop(2)
-        second_hop(3)
+        second_hop(2, whole)
+        second_hop(3, first)
+        second_hop(3, second)

@@ -3,7 +3,7 @@ from contextlib import ExitStack
 import concourse.mybir as mybir
 
 K, T, S, N, H, W = 512, 2048, 256, 512, 512, 1024
-FLOPS = 3 * 2 * 512 * 512 * 256
+FLOPS = 2 * S * (K * H + H * N + K * N)
 
 F32 = mybir.dt.float32
 BF16 = mybir.dt.bfloat16
@@ -18,16 +18,11 @@ COPY = mybir.ActivationFunctionType.Copy
 P = 128
 PACK = 4
 MEMBERS = 4
+LIST_ROWS = 16
+QUADRANT = 32
 Y_WINDOW = 528
-H_WINDOW = 512
+H_WINDOW = 2 * S
 W1_ON_SCALAR = 48
-
-
-def deal(engine_copy, dealt, raw, ms, ts):
-    engine_copy(
-        dealt[:, :, ms, :].rearrange("p t m j -> p m j t"),
-        raw[:].rearrange("p j (m t) -> p m j t", t=PACK)[:, ms, :, ts],
-    )
 
 
 def tile_picked_mixingmidhopmn_none_p_kernel(
@@ -42,22 +37,22 @@ def tile_picked_mixingmidhopmn_none_p_kernel(
         keep = ctx.enter_context(tc.tile_pool(name="keep", bufs=1))
         psum = ctx.enter_context(tc.psum_pool(name="psum", bufs=1))
 
-        offs_t = keep.tile([P, S // 16], U16, name="offs_t")
-        two_t = keep.tile([P, S // 16], U16, name="two_t")
-        n1_t = keep.tile([P, W // 16], U16, name="n1_t")
-        n2_t = keep.tile([P, S // 16], U16, name="n2_t")
-        n3_t = keep.tile([P, S // 16], U16, name="n3_t")
+        offs_t = keep.tile([P, S // LIST_ROWS], U16, name="offs_t")
+        two_t = keep.tile([P, S // LIST_ROWS], U16, name="two_t")
+        n1_t = keep.tile([P, W // LIST_ROWS], U16, name="n1_t")
+        n2_t = keep.tile([P, S // LIST_ROWS], U16, name="n2_t")
+        n3_t = keep.tile([P, S // LIST_ROWS], U16, name="n3_t")
         words = keep.tile([P, T], U32, name="words", align_bytes=64)
         scales = keep.tile([P, T], U8, name="scales", align_bytes=64)
-        w1_raw = keep.tile([P, PACK, H], F32, name="w1_raw", tag="first", align_bytes=64)
+        w1_raw = keep.tile([P, PACK, H], F32, name="w1_raw", tag="w1_then_w3", align_bytes=64)
 
         y_win = [keep.tile([P, Y_WINDOW], F32, name=f"y_win{t}", align_bytes=64) for t in range(PACK)]
         h_win = [keep.tile([P, H_WINDOW], F32, name=f"h_win{t}", align_bytes=64) for t in range(PACK)]
         st_win = [keep.tile([P, H_WINDOW], F32, name=f"st_win{t}", align_bytes=64) for t in range(PACK)]
 
-        scale_rows = keep.tile([P, T], U8, name="scale_rows", tag="small", align_bytes=64)
-        for r in range(4):
-            nc.sync.dma_start(scale_rows[r:P:32, :].bitcast(I32), x_scales[0, r:16:4, :].bitcast(I32))
+        scale_rows = keep.tile([P, T], U8, name="scale_rows", tag="rows_then_gain", align_bytes=64)
+        for r in range(PACK):
+            nc.sync.dma_start(scale_rows[r:P:QUADRANT, :].bitcast(I32), x_scales[0, r:16:PACK, :].bitcast(I32))
         nc.sync.dma_start(offs_t[:], offs)
         nc.sync.dma_start(w1_raw[:], w1.rearrange("(p j) c -> p j c", j=PACK))
         nc.sync.dma_start(two_t[:], two)
@@ -67,29 +62,32 @@ def tile_picked_mixingmidhopmn_none_p_kernel(
         nc.sync.dma_start(n3_t[:], n3)
 
         nc.vector.memset(scales[:].bitcast(I32), 0)
-        for q in range(4):
-            rows = slice(32 * q, 32 * q + 4)
+        for q in range(P // QUADRANT):
+            rows = slice(QUADRANT * q, QUADRANT * q + PACK)
             nc.vector.tensor_copy(scales[rows, :].bitcast(I32), scale_rows[rows, :].bitcast(I32))
-        ps = [keep.tile([P, S], U8, name=f"ps{i}", align_bytes=64) for i in range(2)]
-        nc.vector.tensor_copy(ps[0][:], scales[:].indirect(offs_t[:]))
-        nc.vector.tensor_copy(ps[1][:], scales[:].indirect(two_t[:]))
+        picked_s = [keep.tile([P, S], U8, name=f"picked_s{i}", align_bytes=64) for i in range(2)]
+        nc.vector.tensor_copy(picked_s[0][:], scales[:].indirect(offs_t[:]))
+        nc.vector.tensor_copy(picked_s[1][:], scales[:].indirect(two_t[:]))
 
         for t in range(PACK):
             nc.vector.memset(y_win[t][:, S:], 0.0)
 
-        w1_bf = keep.tile([P, PACK, P, PACK], BF16, name="w1_bf", tag="second", align_bytes=64)
-        deal(scalar_copy, w1_bf, w1_raw, slice(0, W1_ON_SCALAR), slice(0, PACK))
-        deal(nc.vector.tensor_copy, w1_bf, w1_raw, slice(W1_ON_SCALAR, P), slice(0, PACK))
+        w1_bf = keep.tile([P, PACK, P, PACK], BF16, name="w1_bf", tag="w1_bf_then_w2", align_bytes=64)
+        for engine_copy, ms in ((scalar_copy, slice(0, W1_ON_SCALAR)), (nc.vector.tensor_copy, slice(W1_ON_SCALAR, P))):
+            engine_copy(
+                w1_bf[:, :, ms, :].rearrange("p t m j -> p m j t"),
+                w1_raw[:].rearrange("p j (m t) -> p m j t", t=PACK)[:, ms, :, :],
+            )
         w1_c = keep.tile([P, H], U32, name="w1_c", align_bytes=64)
         w1_s = keep.tile([P, H], U8, name="w1_s", align_bytes=64)
         nc.vector.quantize_mx(w1_c[:].bitcast(FP8X4), w1_s[:], w1_bf[:].rearrange("p t m j -> p (t m j)"))
 
-        pw = [keep.tile([P, S], U32, name=f"pw{i}", align_bytes=64) for i in range(2)]
-        nc.vector.tensor_copy(pw[0][:], words[:].indirect(offs_t[:]))
-        nc.vector.tensor_copy(pw[1][:], words[:].indirect(two_t[:]))
+        picked_c = [keep.tile([P, S], U32, name=f"picked_c{i}", align_bytes=64) for i in range(2)]
+        nc.vector.tensor_copy(picked_c[0][:], words[:].indirect(offs_t[:]))
+        nc.vector.tensor_copy(picked_c[1][:], words[:].indirect(two_t[:]))
 
-        w3_raw = keep.tile([P, PACK, N], F32, name="w3_raw", tag="first", align_bytes=64)
-        w2_raw = keep.tile([P, PACK, N], F32, name="w2_raw", tag="second", align_bytes=64)
+        w3_raw = keep.tile([P, PACK, N], F32, name="w3_raw", tag="w1_then_w3", align_bytes=64)
+        w2_raw = keep.tile([P, PACK, N], F32, name="w2_raw", tag="w1_bf_then_w2", align_bytes=64)
         nc.sync.dma_start(w3_raw[:], w3.rearrange("(p j) c -> p j c", j=PACK))
         nc.sync.dma_start(w2_raw[:], w2.rearrange("(p j) c -> p j c", j=PACK))
 
@@ -98,43 +96,43 @@ def tile_picked_mixingmidhopmn_none_p_kernel(
             cols = slice(t * P, (t + 1) * P)
             nc.tensor.matmul_mx(
                 y_ps[t][:], w1_c[:, cols].bitcast(FP8X4), w1_s[:, cols],
-                pw[0][:].bitcast(FP8X4), ps[0][:], start=True, stop=True,
+                picked_c[0][:].bitcast(FP8X4), picked_s[0][:], start=True, stop=True,
             )
         scalar_copy(y_win[0][:, :S], y_ps[0][:])
         for t in range(1, PACK):
             nc.vector.tensor_copy(y_win[t][:, :S], y_ps[t][:])
 
-        gain = keep.tile([P, PACK], F32, name="gain", tag="small", align_bytes=64)
+        gain = keep.tile([P, PACK], F32, name="gain", tag="rows_then_gain", align_bytes=64)
         nc.sync.dma_start(gain[:], gn.rearrange("(p t) o -> p (t o)", t=PACK))
 
+        halves = (slice(0, S // 2), slice(S // 2, S))
         members = [keep.tile([P, S, MEMBERS], F32, name=f"members{t}", align_bytes=64) for t in range(PACK)]
         for t in range(PACK):
-            for i in range(2):
-                nc.scalar.activation(
-                    members[t][:, i * (S // 2) : (i + 1) * (S // 2), :].rearrange("p j a -> p (j a)"),
-                    y_win[t][:].indirect(n1_t[:, i * 32 : (i + 1) * 32]),
-                    COPY,
-                )
+            for js in halves:
+                offsets = n1_t[:, js.start * MEMBERS // LIST_ROWS : js.stop * MEMBERS // LIST_ROWS]
+                scalar_copy(members[t][:, js, :].rearrange("p j a -> p (j a)"), y_win[t][:].indirect(offsets))
 
-        halves = (slice(0, S // 2), slice(S // 2, S))
         lo = [keep.tile([P, S, 2], F32, name=f"lo{t}", align_bytes=64) for t in range(PACK)]
-        hi = [keep.tile([P, S, 2], F32, name=f"hi{t}", align_bytes=64) for t in range(PACK)]
+        hi = [keep.tile([P, S, 2], F32, name=f"hi{t}", tag=f"hi{t}", align_bytes=64) for t in range(PACK)]
         mn = [keep.tile([P, S], F32, name=f"mn{t}", align_bytes=64) for t in range(PACK)]
         mx = [h_win[t][:, S:] for t in range(PACK)]
-        top = [keep.tile([P, S], F32, name=f"top{t}", align_bytes=64) for t in range(PACK)]
+        top = [keep.tile([P, S], F32, name=f"top{t}", tag=f"top{t}", align_bytes=64) for t in range(PACK)]
         u = keep.tile([P, PACK, S], F32, name="u", align_bytes=64)
 
         w_bf, w_c, w_s = {}, {}, {}
 
-        def round_weight(engine_copy, nm, raw, half):
-            w_bf[nm, half] = keep.tile([P, 2, P, PACK], BF16, name=f"{nm}_bf{half}", align_bytes=64)
-            deal(engine_copy, w_bf[nm, half], raw, slice(0, P), slice(2 * half, 2 * half + 2))
+        def round_weight(engine_copy, nm, raw, pair, tag):
+            w_bf[nm, pair] = keep.tile([P, 2, P, PACK], BF16, name=f"{nm}_bf{pair}", tag=tag, align_bytes=64)
+            engine_copy(
+                w_bf[nm, pair][:].rearrange("p e (a i) j -> p e a j i", i=PACK),
+                raw[:].rearrange("p j (a t i) -> p t a j i", t=PACK, i=PACK)[:, 2 * pair : 2 * pair + 2],
+            )
 
-        def quantize_weight(nm, half, tag):
-            w_c[nm, half] = keep.tile([P, 2 * P], U32, name=f"{nm}_c{half}", tag=tag, align_bytes=64)
-            w_s[nm, half] = keep.tile([P, 2 * P], U8, name=f"{nm}_s{half}", align_bytes=64)
+        def quantize_weight(nm, pair, tag):
+            w_c[nm, pair] = keep.tile([P, 2 * P], U32, name=f"{nm}_c{pair}", tag=tag, align_bytes=64)
+            w_s[nm, pair] = keep.tile([P, 2 * P], U8, name=f"{nm}_s{pair}", align_bytes=64)
             nc.vector.quantize_mx(
-                w_c[nm, half][:].bitcast(FP8X4), w_s[nm, half][:], w_bf[nm, half][:].rearrange("p t m j -> p (t m j)")
+                w_c[nm, pair][:].bitcast(FP8X4), w_s[nm, pair][:], w_bf[nm, pair][:].rearrange("p e m j -> p (e m j)")
             )
 
         def pair_min(t, js):
@@ -159,8 +157,8 @@ def tile_picked_mixingmidhopmn_none_p_kernel(
 
         def round_z(i):
             nc.vector.tensor_tensor(
-                z_bf[i][:].rearrange("p (c i) t -> p c t i", i=4),
-                u[:, :, halves[i]].rearrange("p t (c i) -> p c t i", i=4),
+                z_bf[i][:].rearrange("p (c n) t -> p c t n", n=4),
+                u[:, :, halves[i]].rearrange("p t (c n) -> p c t n", n=4),
                 gain[:].unsqueeze(1).unsqueeze(3).to_broadcast([P, S // 8, PACK, 4]),
                 ALU.mult,
             )
@@ -169,24 +167,22 @@ def tile_picked_mixingmidhopmn_none_p_kernel(
             nc.vector.quantize_mx(z_c[i][:].bitcast(FP8X4), z_s[i][:], z_bf[i][:].rearrange("p j t -> p (j t)"))
 
         whole = slice(0, S)
+        first, second = halves
         last = PACK - 1
         for t in range(last):
-            pair_min(t, halves[0])
-            pair_max(t, halves[0])
-            if t == 0:
-                round_weight(nc.vector.tensor_copy, "w3", w3_raw, 0)
-            else:
+            pair_min(t, first)
+            pair_max(t, first)
+            if t > 0:
                 combine(t - 1, whole)
-            pair_min(t, halves[1])
-            pair_max(t, halves[1])
-            if t == 0:
-                quantize_weight("w3", 0, "w3_c0")
+            pair_min(t, second)
+            pair_max(t, second)
             extremes(t, whole)
             larger(t, whole)
-        round_weight(scalar_copy, "w2", w2_raw, 0)
-        round_weight(scalar_copy, "w3", w3_raw, 1)
-        round_weight(scalar_copy, "w2", w2_raw, 1)
-        first, second = halves
+
+        round_weight(nc.scalar.copy, "w3", w3_raw, 0, "w3_bf0")
+        round_weight(nc.scalar.copy, "w2", w2_raw, 0, "w2_bf0")
+        round_weight(nc.scalar.copy, "w3", w3_raw, 1, "w3_bf1")
+
         pair_min(last, first)
         pair_max(last, first)
         combine(last - 1, whole)
@@ -200,23 +196,24 @@ def tile_picked_mixingmidhopmn_none_p_kernel(
         larger(last, second)
         quantize_z(0)
         combine(last, second)
-        quantize_weight("w2", 0, "w2_c")
+        quantize_weight("w3", 0, f"hi{last}")
         round_z(1)
+        quantize_weight("w2", 0, f"top{last}")
         quantize_z(1)
 
-        out_rows = out.rearrange("(p t) j -> p t j", t=PACK)
+        out_rows = out.rearrange("(a t i) j -> t a i j", t=PACK, i=PACK)
         h_ps = [psum.tile([P, S], F32, name=f"h_ps{t}") for t in range(PACK)]
 
         def product(t):
-            half = t // 2
+            pair = t // 2
             cols = slice((t % 2) * P, (t % 2 + 1) * P)
             nc.tensor.matmul_mx(
-                h_ps[t][:], w_c["w3", half][:, cols].bitcast(FP8X4), w_s["w3", half][:, cols],
-                pw[1][:].bitcast(FP8X4), ps[1][:], start=True, stop=False,
+                h_ps[t][:], w_c["w3", pair][:, cols].bitcast(FP8X4), w_s["w3", pair][:, cols],
+                picked_c[1][:].bitcast(FP8X4), picked_s[1][:], start=True, stop=False,
             )
             for i in range(2):
                 nc.tensor.matmul_mx(
-                    h_ps[t][:, halves[i]], w_c["w2", half][:, cols].bitcast(FP8X4), w_s["w2", half][:, cols],
+                    h_ps[t][:, halves[i]], w_c["w2", pair][:, cols].bitcast(FP8X4), w_s["w2", pair][:, cols],
                     z_c[i][:].bitcast(FP8X4), z_s[i][:], start=False, stop=(i == 1),
                 )
             nc.vector.tensor_copy(h_win[t][:, :S], h_ps[t][:])
@@ -226,27 +223,28 @@ def tile_picked_mixingmidhopmn_none_p_kernel(
         res = [keep.tile([P, S], F32, name=f"res{t}", align_bytes=64) for t in range(PACK)]
 
         def first_hop(t):
-            nc.scalar.activation(h_at[t], h_win[t][:].indirect(n2_t[:]), COPY)
+            scalar_copy(h_at[t], h_win[t][:].indirect(n2_t[:]))
             nc.vector.tensor_tensor(st_win[t][:, :S], h_win[t][:, :S], h_at[t], ALU.max)
 
         def second_hop(t, js):
-            offsets = n3_t[:, js.start // 16 : js.stop // 16]
-            nc.scalar.activation(st_at[t][:, js], st_win[t][:].indirect(offsets), COPY)
+            offsets = n3_t[:, js.start // LIST_ROWS : js.stop // LIST_ROWS]
+            scalar_copy(st_at[t][:, js], st_win[t][:].indirect(offsets))
             nc.vector.tensor_tensor(res[t][:, js], st_win[t][:, js], st_at[t][:, js], ALU.min)
-            nc.sync.dma_start(out_rows[:, t, js], res[t][:, js])
+            nc.sync.dma_start(out_rows[t][:, :, js], res[t][:, js])
 
         quantize_weight("w3", 1, "z_bf1")
         product(0)
         product(1)
-        quantize_weight("w2", 1, "w2_c")
+        round_weight(nc.vector.tensor_copy, "w2", w2_raw, 1, f"top{last}")
         first_hop(0)
-        product(2)
+        quantize_weight("w2", 1, "w2_c1")
         first_hop(1)
+        product(2)
         product(3)
         second_hop(0, whole)
-        first_hop(2)
         second_hop(1, whole)
+        first_hop(2)
         first_hop(3)
         second_hop(2, whole)
-        second_hop(3, first)
-        second_hop(3, second)
+        second_hop(last, first)
+        second_hop(last, second)

from contextlib import ExitStack

import concourse.mybir as mybir

K, T, S, N, H, W = 512, 2048, 256, 512, 512, 1024
FLOPS = 2 * S * (K * H + H * N + K * N)

F32 = mybir.dt.float32
BF16 = mybir.dt.bfloat16
I32 = mybir.dt.int32
U32 = mybir.dt.uint32
U16 = mybir.dt.uint16
U8 = mybir.dt.uint8
FP8X4 = mybir.dt.float8_e4m3fn_x4
ALU = mybir.AluOpType
COPY = mybir.ActivationFunctionType.Copy

P = 128
PACK = 4
MEMBERS = 4
LIST_ROWS = 16
QUADRANT = 32
Y_WINDOW = 528
H_WINDOW = 2 * S
W1_ON_SCALAR = 48


def tile_picked_mixingmidhopmn_none_p_kernel(
    tc, x_words, x_scales, w1, gn, w2, w3, offs, n1, two, n2, n3, out
):
    nc = tc.nc

    def scalar_copy(dst, src):
        nc.scalar.activation(dst, src, COPY)

    with ExitStack() as ctx:
        keep = ctx.enter_context(tc.tile_pool(name="keep", bufs=1))
        psum = ctx.enter_context(tc.psum_pool(name="psum", bufs=1))

        offs_t = keep.tile([P, S // LIST_ROWS], U16, name="offs_t")
        two_t = keep.tile([P, S // LIST_ROWS], U16, name="two_t")
        n1_t = keep.tile([P, W // LIST_ROWS], U16, name="n1_t")
        n2_t = keep.tile([P, S // LIST_ROWS], U16, name="n2_t")
        n3_t = keep.tile([P, S // LIST_ROWS], U16, name="n3_t")
        words = keep.tile([P, T], U32, name="words", align_bytes=64)
        scales = keep.tile([P, T], U8, name="scales", align_bytes=64)
        w1_raw = keep.tile([P, PACK, H], F32, name="w1_raw", tag="w1_then_w3", align_bytes=64)

        y_win = [keep.tile([P, Y_WINDOW], F32, name=f"y_win{t}", align_bytes=64) for t in range(PACK)]
        h_win = [keep.tile([P, H_WINDOW], F32, name=f"h_win{t}", align_bytes=64) for t in range(PACK)]
        st_win = [keep.tile([P, H_WINDOW], F32, name=f"st_win{t}", align_bytes=64) for t in range(PACK)]

        scale_rows = keep.tile([P, T], U8, name="scale_rows", tag="rows_then_gain", align_bytes=64)
        for r in range(PACK):
            nc.sync.dma_start(scale_rows[r:P:QUADRANT, :].bitcast(I32), x_scales[0, r:16:PACK, :].bitcast(I32))
        nc.sync.dma_start(offs_t[:], offs)
        nc.sync.dma_start(w1_raw[:], w1.rearrange("(p j) c -> p j c", j=PACK))
        nc.sync.dma_start(two_t[:], two)
        nc.sync.dma_start(words[:].bitcast(I32), x_words[0].rearrange("p n t -> p (n t)").bitcast(I32))
        nc.sync.dma_start(n1_t[:], n1)
        nc.sync.dma_start(n2_t[:], n2)
        nc.sync.dma_start(n3_t[:], n3)

        nc.vector.memset(scales[:].bitcast(I32), 0)
        for q in range(P // QUADRANT):
            rows = slice(QUADRANT * q, QUADRANT * q + PACK)
            nc.vector.tensor_copy(scales[rows, :].bitcast(I32), scale_rows[rows, :].bitcast(I32))
        picked_s = [keep.tile([P, S], U8, name=f"picked_s{i}", align_bytes=64) for i in range(2)]
        nc.vector.tensor_copy(picked_s[0][:], scales[:].indirect(offs_t[:]))
        nc.vector.tensor_copy(picked_s[1][:], scales[:].indirect(two_t[:]))

        for t in range(PACK):
            nc.vector.memset(y_win[t][:, S:], 0.0)

        w1_bf = keep.tile([P, PACK, P, PACK], BF16, name="w1_bf", tag="w1_bf_then_w2", align_bytes=64)
        for engine_copy, ms in ((scalar_copy, slice(0, W1_ON_SCALAR)), (nc.vector.tensor_copy, slice(W1_ON_SCALAR, P))):
            engine_copy(
                w1_bf[:, :, ms, :].rearrange("p t m j -> p m j t"),
                w1_raw[:].rearrange("p j (m t) -> p m j t", t=PACK)[:, ms, :, :],
            )
        w1_c = keep.tile([P, H], U32, name="w1_c", align_bytes=64)
        w1_s = keep.tile([P, H], U8, name="w1_s", align_bytes=64)
        nc.vector.quantize_mx(w1_c[:].bitcast(FP8X4), w1_s[:], w1_bf[:].rearrange("p t m j -> p (t m j)"))

        picked_c = [keep.tile([P, S], U32, name=f"picked_c{i}", align_bytes=64) for i in range(2)]
        nc.vector.tensor_copy(picked_c[0][:], words[:].indirect(offs_t[:]))
        nc.vector.tensor_copy(picked_c[1][:], words[:].indirect(two_t[:]))

        w3_raw = keep.tile([P, PACK, N], F32, name="w3_raw", tag="w1_then_w3", align_bytes=64)
        w2_raw = keep.tile([P, PACK, N], F32, name="w2_raw", tag="w1_bf_then_w2", align_bytes=64)
        nc.sync.dma_start(w3_raw[:], w3.rearrange("(p j) c -> p j c", j=PACK))
        nc.sync.dma_start(w2_raw[:], w2.rearrange("(p j) c -> p j c", j=PACK))

        y_ps = [psum.tile([P, S], F32, name=f"y_ps{t}") for t in range(PACK)]
        for t in range(PACK):
            cols = slice(t * P, (t + 1) * P)
            nc.tensor.matmul_mx(
                y_ps[t][:], w1_c[:, cols].bitcast(FP8X4), w1_s[:, cols],
                picked_c[0][:].bitcast(FP8X4), picked_s[0][:], start=True, stop=True,
            )
        scalar_copy(y_win[0][:, :S], y_ps[0][:])
        for t in range(1, PACK):
            nc.vector.tensor_copy(y_win[t][:, :S], y_ps[t][:])

        gain = keep.tile([P, PACK], F32, name="gain", tag="rows_then_gain", align_bytes=64)
        nc.sync.dma_start(gain[:], gn.rearrange("(p t) o -> p (t o)", t=PACK))

        halves = (slice(0, S // 2), slice(S // 2, S))
        members = [keep.tile([P, S, MEMBERS], F32, name=f"members{t}", align_bytes=64) for t in range(PACK)]
        for t in range(PACK):
            for js in halves:
                offsets = n1_t[:, js.start * MEMBERS // LIST_ROWS : js.stop * MEMBERS // LIST_ROWS]
                scalar_copy(members[t][:, js, :].rearrange("p j a -> p (j a)"), y_win[t][:].indirect(offsets))

        lo = [keep.tile([P, S, 2], F32, name=f"lo{t}", align_bytes=64) for t in range(PACK)]
        hi = [keep.tile([P, S, 2], F32, name=f"hi{t}", tag=f"hi{t}", align_bytes=64) for t in range(PACK)]
        mn = [keep.tile([P, S], F32, name=f"mn{t}", align_bytes=64) for t in range(PACK)]
        mx = [h_win[t][:, S:] for t in range(PACK)]
        top = [keep.tile([P, S], F32, name=f"top{t}", tag=f"top{t}", align_bytes=64) for t in range(PACK)]
        u = keep.tile([P, PACK, S], F32, name="u", align_bytes=64)

        w_bf, w_c, w_s = {}, {}, {}

        def round_weight(engine_copy, nm, raw, pair, tag):
            w_bf[nm, pair] = keep.tile([P, 2, P, PACK], BF16, name=f"{nm}_bf{pair}", tag=tag, align_bytes=64)
            engine_copy(
                w_bf[nm, pair][:].rearrange("p e (a i) j -> p e a j i", i=PACK),
                raw[:].rearrange("p j (a t i) -> p t a j i", t=PACK, i=PACK)[:, 2 * pair : 2 * pair + 2],
            )

        def quantize_weight(nm, pair, tag):
            w_c[nm, pair] = keep.tile([P, 2 * P], U32, name=f"{nm}_c{pair}", tag=tag, align_bytes=64)
            w_s[nm, pair] = keep.tile([P, 2 * P], U8, name=f"{nm}_s{pair}", align_bytes=64)
            nc.vector.quantize_mx(
                w_c[nm, pair][:].bitcast(FP8X4), w_s[nm, pair][:], w_bf[nm, pair][:].rearrange("p e m j -> p (e m j)")
            )

        def pair_min(t, js):
            nc.vector.tensor_tensor(lo[t][:, js, :], members[t][:, js, 0:2], members[t][:, js, 2:4], ALU.min)

        def pair_max(t, js):
            nc.vector.tensor_tensor(hi[t][:, js, :], members[t][:, js, 0:2], members[t][:, js, 2:4], ALU.max)

        def extremes(t, js):
            nc.vector.tensor_tensor(mn[t][:, js], lo[t][:, js, 0], lo[t][:, js, 1], ALU.min)
            nc.vector.tensor_tensor(mx[t][:, js], hi[t][:, js, 0], hi[t][:, js, 1], ALU.max)

        def larger(t, js):
            nc.vector.tensor_tensor(top[t][:, js], mn[t][:, js], y_win[t][:, js], ALU.max)

        def combine(t, js):
            nc.vector.scalar_tensor_tensor(u[:, t, js], mx[t][:, js], -0.5, top[t][:, js], ALU.mult, ALU.add)

        z_bf = [keep.tile([P, S // 2, PACK], BF16, name=f"z_bf{i}", tag=f"z_bf{i}", align_bytes=64) for i in range(2)]
        z_c = [keep.tile([P, S // 2], U32, name=f"z_c{i}", align_bytes=64) for i in range(2)]
        z_s = [keep.tile([P, S // 2], U8, name=f"z_s{i}", align_bytes=64) for i in range(2)]

        def round_z(i):
            nc.vector.tensor_tensor(
                z_bf[i][:].rearrange("p (c n) t -> p c t n", n=4),
                u[:, :, halves[i]].rearrange("p t (c n) -> p c t n", n=4),
                gain[:].unsqueeze(1).unsqueeze(3).to_broadcast([P, S // 8, PACK, 4]),
                ALU.mult,
            )

        def quantize_z(i):
            nc.vector.quantize_mx(z_c[i][:].bitcast(FP8X4), z_s[i][:], z_bf[i][:].rearrange("p j t -> p (j t)"))

        whole = slice(0, S)
        first, second = halves
        last = PACK - 1
        for t in range(last):
            pair_min(t, first)
            pair_max(t, first)
            if t > 0:
                combine(t - 1, whole)
            pair_min(t, second)
            pair_max(t, second)
            extremes(t, whole)
            larger(t, whole)

        round_weight(nc.scalar.copy, "w3", w3_raw, 0, "w3_bf0")
        round_weight(nc.scalar.copy, "w2", w2_raw, 0, "w2_bf0")
        round_weight(nc.scalar.copy, "w3", w3_raw, 1, "w3_bf1")

        pair_min(last, first)
        pair_max(last, first)
        combine(last - 1, whole)
        extremes(last, first)
        pair_min(last, second)
        larger(last, first)
        pair_max(last, second)
        combine(last, first)
        extremes(last, second)
        round_z(0)
        larger(last, second)
        quantize_z(0)
        combine(last, second)
        quantize_weight("w3", 0, f"hi{last}")
        round_z(1)
        quantize_weight("w2", 0, f"top{last}")
        quantize_z(1)

        out_rows = out.rearrange("(a t i) j -> t a i j", t=PACK, i=PACK)
        h_ps = [psum.tile([P, S], F32, name=f"h_ps{t}") for t in range(PACK)]

        def product(t):
            pair = t // 2
            cols = slice((t % 2) * P, (t % 2 + 1) * P)
            nc.tensor.matmul_mx(
                h_ps[t][:], w_c["w3", pair][:, cols].bitcast(FP8X4), w_s["w3", pair][:, cols],
                picked_c[1][:].bitcast(FP8X4), picked_s[1][:], start=True, stop=False,
            )
            for i in range(2):
                nc.tensor.matmul_mx(
                    h_ps[t][:, halves[i]], w_c["w2", pair][:, cols].bitcast(FP8X4), w_s["w2", pair][:, cols],
                    z_c[i][:].bitcast(FP8X4), z_s[i][:], start=False, stop=(i == 1),
                )
            nc.vector.tensor_copy(h_win[t][:, :S], h_ps[t][:])

        h_at = [st_win[t][:, S:] for t in range(PACK)]
        st_at = [keep.tile([P, S], F32, name=f"st_at{t}", align_bytes=64) for t in range(PACK)]
        res = [keep.tile([P, S], F32, name=f"res{t}", align_bytes=64) for t in range(PACK)]

        def first_hop(t):
            scalar_copy(h_at[t], h_win[t][:].indirect(n2_t[:]))
            nc.vector.tensor_tensor(st_win[t][:, :S], h_win[t][:, :S], h_at[t], ALU.max)

        def second_hop(t, js):
            offsets = n3_t[:, js.start // LIST_ROWS : js.stop // LIST_ROWS]
            scalar_copy(st_at[t][:, js], st_win[t][:].indirect(offsets))
            nc.vector.tensor_tensor(res[t][:, js], st_win[t][:, js], st_at[t][:, js], ALU.min)
            nc.sync.dma_start(out_rows[t][:, :, js], res[t][:, js])

        quantize_weight("w3", 1, "z_bf1")
        product(0)
        product(1)
        round_weight(nc.vector.tensor_copy, "w2", w2_raw, 1, f"top{last}")
        first_hop(0)
        quantize_weight("w2", 1, "w2_c1")
        first_hop(1)
        product(2)
        product(3)
        second_hop(0, whole)
        second_hop(1, whole)
        first_hop(2)
        first_hop(3)
        second_hop(2, whole)
        second_hop(last, first)
        second_hop(last, second)
